import numpy as np
CORES = [71,199,95,223,103,231,111,239,119,247,127,255]
N = 12
R, E = 4096, 1024
CAPP = 256
def entries(a): return a.T.reshape(-1)
def pack(v, P): return np.ascontiguousarray(np.asarray(v, np.int32).reshape(-1, P).T)
def lists(rng, how):
    n = N * E; q = np.arange(n) // E
    P = rng.permutation(np.repeat(np.arange(N * N), CAPP))[:n]
    if how == "full":
        a = rng.integers(0, N); z = np.delete(np.arange(N), a); o = rng.permutation(N * N); o = o[(o // N != a) & (o % N != a) & (o // N != o % N)]
        C = np.concatenate([N * a + rng.permutation(z), [(N + 1) * a], N * rng.permutation(z) + a, o])[:n // CAPP]
        L = np.repeat(C, CAPP).reshape(N, E); s, t = 1 + 2 * rng.integers(0, CAPP // 8, 2); t += 2 * (CAPP // 8)
        L[0, :s], L[1, :s] = C[E // CAPP], C[0]; L[0, s:s + t], L[N - 1, E - t:] = C[-1], C[0]
        L = L[rng.permutation(N)]; L[0] = L[0].reshape(16, -1).T.reshape(-1)
        for r in range(1, N, 2): L[r] = rng.permutation(L[r])
        P = L.reshape(-1)
    if how == "same":
        o = np.arange(N * N); o = rng.permutation(np.repeat(o[o % (N + 1) != 0], CAPP))[:n - N * CAPP].reshape(N, E - CAPP)
        P = np.stack([rng.permutation(np.append(o[r], np.full(CAPP, (N + 1) * r))) for r in range(N)]).reshape(-1)
    if how == "cross":
        d = np.stack([rng.permutation(1 + np.arange(E) % (N - 1)) for r in range(N)]).reshape(-1); a = 1 + rng.integers(0, N - 2, N); a += a >= N - np.arange(N)
        P = (q + a[d]) % N * N + (q + a[d] + d) % N
    if how == "edge": k = rng.permutation(n); P = k % (N * N)
    h, g = P // N, P % N; u, v = rng.integers(0, R, n), rng.integers(0, R, n)
    if how == "alike": u, v = rng.integers(0, R, N * N)[P], rng.integers(0, R, N * N)[P]
    if how == "edge": u, v = (R - 1) * (k // (N * N) % 2), (R - 1) * (k // (2 * N * N) % 2)
    if how == "full": u, v = (np.stack([rng.permutation(R)[np.arange(E) % R] for r in range(N)]).reshape(-1) for _ in range(2))
    if how == "same": v = u
    return {"pi": np.stack([pack(w, 16) for w in (R * h + u).reshape(N, E)]), "pj": np.stack([pack(w, 16) for w in (R * g + v).reshape(N, E)])}
def setup_inputs(rng):
    return dict({"ta": rng.standard_normal((N, 128, R), dtype=np.float32), "tb": rng.standard_normal((N, 128, R), dtype=np.float32)}, **lists(rng, "uniform"))
def setup_inputs_alike(rng):
    d = setup_inputs(rng); d.update(lists(rng, "alike"))
    for k in ("ta", "tb"): d[k] = (d[k].astype(np.float32) * 1024.0).astype(d[k].dtype)
    return d
def setup_inputs_cross(rng):
    d = setup_inputs(rng); d.update(lists(rng, "cross"))
    for k in ("ta", "tb"): d[k] = (d[k].astype(np.float32) * (1 / 1024.0)).astype(d[k].dtype)
    return d
def setup_inputs_edge(rng):
    d = setup_inputs(rng); d.update(lists(rng, "edge"))
    return d
def setup_inputs_full(rng):
    d = setup_inputs(rng); d.update(lists(rng, "full"))
    return d
def setup_inputs_same(rng):
    d = setup_inputs(rng); d.update(lists(rng, "same"))
    return d
def check_inputs(x):
    bad = []
    if x["pi"].min() < 0 or x["pi"].max() >= N * R: bad.append("pi out of range")
    if x["pj"].min() < 0 or x["pj"].max() >= N * R: bad.append("pj out of range")
    if not bad and int(np.bincount((x["pi"] // R * N + x["pj"] // R).reshape(-1), minlength=N * N).max()) > CAPP: bad.append("more than CAPP pairs with i in one rank's part of TA and j in one rank's part of TB")
    return bad
def reference(ta, tb, pi, pj):
    A, B = np.concatenate(list(ta), axis=1).astype(np.float64), np.concatenate(list(tb), axis=1).astype(np.float64)
    y = []
    for r in range(N):
        i, j = entries(pi[r]), entries(pj[r])
        y.append((A[:, i] * B[:, j]).sum(axis=0))
    return {"y": np.stack(y).reshape(N, -1, 16).transpose(0, 2, 1).astype(np.float32)}

@@ -1,0 +1,376 @@
+from concourse.bass import DstId, RemoteDMATransfer
+from concourse.mybir import AluOpType as Op
+from concourse.mybir import ActivationFunctionType as Fn
+
+N = 12
+C = 96
+S = 256
+BLK = 3
+WORLD = 256
+STRAIGHT = ((2, 10), (4, 8, 1, 11))
+HELPED = ((3, 9), (5, 7, 6))
+
+SCRATCH = {
+    "LAND": ("dram", [N, 128, 16], "int32"),
+    "RET": ("dram", [N, 128, 8], "float32"),
+    "BACK": ("dram", [N, 128, 8], "float32"),
+    "TAS": ("sbuf", [128, 4096], "float32"),
+    "TBS": ("sbuf", [128, 4096], "float32"),
+    "L": ("sbuf", [128, 192], "int32"),
+    "HG": ("sbuf", [128, 192], "int32"),
+    "UV": ("sbuf", [128, 192], "int32"),
+    "VAL": ("sbuf", [128, 192], "float32"),
+    "NOT": ("sbuf", [128, 192], "float16"),
+    "KEY": ("sbuf", [128, C], "float16"),
+    "MR": ("sbuf", [128, 2 * N * C], "float16"),
+    "SC": ("sbuf", [128, N * C], "float16"),
+    "PROD": ("sbuf", [128, N * C], "float16"),
+    "T1": ("sbuf", [128, C], "float32"),
+    "ROW": ("sbuf", [128, C], "float32"),
+    "HOT": ("sbuf", [128, C * 128], "float16"),
+    "PF": ("sbuf", [128, 24], "float16"),
+    "OA": ("sbuf", [128, 192], "uint16"),
+    "OB": ("sbuf", [128, 288], "uint16"),
+    "DF": ("sbuf", [128, C], "float32"),
+    "DG": ("sbuf", [128, C], "float32"),
+    "COL": ("sbuf", [128, 11 * S], "float32"),
+    "FWD": ("sbuf", [128, 5 * S], "float32"),
+    "RECV": ("sbuf", [128, N * S], "float32"),
+    "PR": ("sbuf", [128, N * S], "float32"),
+    "WIN": ("sbuf", [128, N * S + 8], "float32"),
+    "D": ("sbuf", [128, 16 * C], "float32"),
+    "FIN": ("sbuf", [24, 512], "float32"),
+    "Y": ("sbuf", [32, 32], "float32"),
+    "IOF": ("sbuf", [128, 128], "float32"),
+    "IOH": ("sbuf", [128, 128], "float16"),
+    "PK": ("sbuf", [128, 8], "float32"),
+    "MODF": ("sbuf", [128, 128], "float32"),
+    "SEGF": ("sbuf", [128, 4 * C], "float32"),
+    "SEG": ("sbuf", [128, 4 * C], "float16"),
+    "PI1": ("sbuf", [128, 1], "int32"),
+    "PI2": ("sbuf", [128, 1], "int32"),
+    "PF2": ("sbuf", [128, 1], "float32"),
+    "TM": ("sbuf", [128, 128], "float16"),
+    "ONEH": ("sbuf", [128, 128], "float16"),
+    "ID": ("sbuf", [128, 128], "float16"),
+    "WK": ("sbuf", [128, 8 * 128], "float16"),
+    "IDX": ("sbuf", [128, N * 128], "float16"),
+    "ONE32": ("sbuf", [128, 128], "float32"),
+    "Z": ("sbuf", [128, 48], "float32"),
+}
+for _i in range(8):
+    SCRATCH["ps%d" % _i] = ("psum", [128, 512], "float32")
+
+SEMAPHORES = (["v", "t", "a", "gi", "own", "lst", "lsx", "ld", "lta", "ltb", "ob", "ls", "bk", "back", "fin", "st"]
+              + ["rd%d" % j for j in range(BLK)] + ["fw%d" % k for k in range(len(HELPED))] + ["col%d" % a for a in range(N)])
+
+
+def bits(mask):
+    return [e for e in range(16) if mask >> e & 1]
+
+
+def mask_of(engines):
+    m = 0
+    for e in engines:
+        m |= 1 << e
+    return m
+
+
+def same_chip(a, b, topo):
+    return topo.host(a) == topo.host(b) and topo.chip(a) == topo.chip(b)
+
+
+def helper(x, cores, topo):
+    for c in range(WORLD):
+        if same_chip(c, x, topo) and topo.die(c) != topo.die(x) and all(topo.may_write(c, d) for d in cores if d != c):
+            return c
+
+
+def shares(n):
+    return {1: (1,), 2: (2, 2), 3: (2, 4, 4), 4: (4, 4, 4, 4)}[n]
+
+
+def split(engines, n):
+    out, at = [], 0
+    for s in shares(n):
+        k = len(engines) // s
+        out.append(engines[at:at + k])
+        at += k
+    return out
+
+
+def rank_program(g, core, T, topo):
+    cores = list(T.cores)
+    me = None
+    for q, x in enumerate(cores):
+        if same_chip(core, x, topo):
+            if core == x:
+                me = ("X", q)
+            elif core == helper(x, cores, topo):
+                me = ("P", q)
+    if me is None:
+        return
+    kind, r = me
+    X = cores
+    P = [helper(x, cores, topo) for x in cores]
+    far = next(x for x in X if not same_chip(x, core, topo))
+    off_chip = bits(topo.mask(core, far))
+    on_chip = bits(topo.mask(core, P[r] if kind == "X" else X[r]))
+    inner = [e for e in on_chip if e not in off_chip]
+    ve, pe, sc, sy = g.vector, g.tensor, g.scalar, g.sync
+    n = {"v": 0, "t": 0, "a": 0, "ls": 0}
+
+    def v(ins):
+        n["v"] += 1
+        ins.then_inc(T.sem.v, 1)
+        return n["v"]
+
+    def t(ins):
+        n["t"] += 1
+        ins.then_inc(T.sem.t, 1)
+        return n["t"]
+
+    def a(ins):
+        n["a"] += 1
+        ins.then_inc(T.sem.a, 1)
+        return n["a"]
+
+    def vw():
+        ve.wait_ge(T.sem.v, n["v"])
+
+    def dst(d):
+        rid, pid = topo.addr(d, core)
+        return DstId(rid=rid, pnc=pid)
+
+    def write(out, src, d, sem, engines):
+        rid, pid = topo.addr(d, core)
+        g.remote_dma(out, src, T.sem[sem], T.sem.ls, pid, rid, mask_of(engines))
+        n["ls"] += len(engines)
+
+    def cast(src, dests, out, sem, engines):
+        g.remote_dma_fused([RemoteDMATransfer(src=src, dsts=[out for d in dests], dst_ids=[dst(d) for d in dests],
+                                              dma_engine_mask=mask_of(engines), remote_sem=T.sem[sem])], local_sem=T.sem.ls)
+        n["ls"] += len(engines)
+
+    if kind == "X":
+        sy.dma_start(T.LAND[r, 0:128:2, :], T.pi[:]).then_inc(T.sem.own, 16)
+        sc.dma_start(T.LAND[r, 1:128:2, :], T.pj[:]).then_inc(T.sem.own, 16)
+    F = {"allow_small_or_imprecise_dtypes": True}
+    g.iota(T.IOF[:], [[1, 128]], 0, 0, **F).then_inc(T.sem.gi, 1)
+    g.iota(T.PK[:], [[-16, 8]], 0, 1, **F).then_inc(T.sem.gi, 1)
+    g.iota(T.MODF[:], [[0, 8], [1, 16]], 0, 0, **F).then_inc(T.sem.gi, 1)
+    g.iota(T.PI1[:], [[0, 1]], 0, 1).then_inc(T.sem.gi, 1)
+    if kind == "X":
+        g.wait_ge(T.sem.own, 32)
+        cast(T.LAND[r], [x for x in X if x != core], T.LAND[r], "lst", off_chip)
+        write(T.LAND[r], T.LAND[r], P[r], "lsx", inner)
+        mine, count = "own", 32
+    else:
+        g.wait_ge(T.sem.lsx, len(inner))
+        cast(T.LAND[r], [p for p in P if p != core], T.LAND[r], "lst", off_chip)
+        mine, count = "lsx", len(inner)
+    g.iota(T.SEGF[:], [[0, 4], [1, C]], 0, 0, **F).then_inc(T.sem.gi, 1)
+    for q in (sy, sc):
+        q.wait_ge(T.sem[mine], count)
+        q.wait_ge(T.sem.lst, (N - 1) * len(off_chip))
+    for j in range(BLK):
+        (sy, sc, sy)[j].dma_start(T.L[:, 64 * j:64 * j + 64], T.LAND[4 * j:4 * j + 4]).then_inc(T.sem.ld, 16)
+    if kind == "X":
+        sy.wait_ge(T.sem.ld, 16 * BLK)
+        sy.dma_start(T.TAS[:], T.ta[:]).then_inc(T.sem.lta, 16)
+        sy.dma_start(T.TBS[:], T.tb[:]).then_inc(T.sem.ltb, 16)
+
+    ve.wait_ge(T.sem.gi, 5)
+    part = T.PK[:, 0:1]
+    v(ve.tensor_copy(T.IOH[:], T.IOF[:]))
+    v(ve.tensor_scalar(T.SEG[:], T.SEGF[:], 0.0, None, Op.is_gt))
+    v(ve.tensor_scalar(T.TM[:], T.IOF[:], part, -1.0, Op.is_le, Op.mult))
+    v(ve.tensor_scalar(T.ONEH[:], T.IOF[:], 0.0, None, Op.is_ge))
+    v(ve.tensor_scalar(T.ID[:], T.IOF[:], part, None, Op.is_equal))
+    for k in range(8):
+        v(ve.tensor_scalar(T.WK[:, 128 * k:128 * k + 128], T.MODF[:], T.PK[:, k:k + 1], None, Op.is_equal))
+    if kind == "X":
+        v(ve.memset(T.ONE32[:], 1.0))
+        v(ve.memset(T.WIN[:, N * S:N * S + 8], 0.0))
+        v(ve.tensor_scalar(T.PI2[:], T.PI1[:], 1, None, Op.bitwise_and))
+        vw()
+        v(ve.tensor_scalar(T.PF2[:], T.PI2[:], 16.0, 15.0, Op.mult, Op.add))
+        vw()
+        v(ve.tensor_scalar(T.Z[:], T.IOF[:, 0:48], T.PF2[:, 0:1], None, Op.is_equal))
+    else:
+        for x in range(N):
+            v(ve.tensor_scalar(T.IDX[:, 128 * x:128 * x + 128], T.IOF[:], part, float(S * x - S * N), Op.is_equal, Op.mult))
+
+    this, other = (0, 16) if kind == "X" else (16, 0)
+    ve.wait_ge(T.sem.ld, 16 * BLK)
+    v(ve.tensor_scalar(T.HG[:], T.L[:], 12, None, Op.arith_shift_right))
+    v(ve.tensor_scalar(T.UV[:], T.L[:], 4095, None, Op.bitwise_and))
+    ve.wait_ge(T.sem.v, n["v"] - 1)
+    v(ve.tensor_scalar(T.NOT[:], T.HG[:], float(r), 16.0, Op.not_equal, Op.mult))
+    vw()
+    for k in range(6):
+        v(ve.tensor_tensor(T.KEY[:, 16 * k:16 * k + 16], T.HG[:, 32 * k + other:32 * k + other + 16],
+                           T.NOT[:, 32 * k + this:32 * k + this + 16], Op.add))
+    vw()
+    W3 = 4 * C
+    masked, scanned, placed, chosen = [], [], [], []
+
+    def masks(i):
+        for x in range(4 * i, 4 * i + 4):
+            v(ve.tensor_scalar(T.MR[:, C * x:C * x + C], T.KEY[:], float(x), None, Op.is_equal))
+        masked.append(n["v"])
+
+    def scan(i):
+        ve.wait_ge(T.sem.v, masked[i])
+        scanned.append(v(ve.tensor_tensor_scan(T.SC[:, W3 * i:W3 * i + W3], T.SEG[:], T.MR[:, W3 * i:W3 * i + W3], 0.0, Op.mult, Op.add)))
+
+    masks(0), masks(1), scan(0), masks(2), scan(1), scan(2)
+    v(ve.tensor_scalar(T.VAL[:], T.UV[:], -2048.0, None, Op.add))
+    pos = [T.ps0, T.ps1, T.ps2]
+    for i in range(3):
+        pe.wait_ge(T.sem.v, masked[i])
+        t(pe.matmul(pos[i][:, 0:W3], T.TM[:], T.MR[:, W3 * i:W3 * i + W3], True, False))
+        pe.wait_ge(T.sem.v, scanned[i])
+        placed.append(t(pe.matmul(pos[i][:, 0:W3], T.ONEH[:], T.SC[:, W3 * i:W3 * i + W3], False, True)))
+    for i in range(3):
+        ve.wait_ge(T.sem.t, placed[i])
+        chosen.append(v(ve.tensor_tensor(T.PROD[:, W3 * i:W3 * i + W3], T.MR[:, W3 * i:W3 * i + W3], pos[i][:, 0:W3], Op.mult)))
+    if kind == "P":
+        for x in range(N):
+            t(pe.matmul(T.ps6[:, 0:C], T.IDX[:, 128 * x:128 * x + 128], T.MR[:, C * x:C * x + C], x == 0, x == N - 1))
+    for x in range(N):
+        if x % 4 == 0:
+            pe.wait_ge(T.sem.v, chosen[x // 4])
+        t(pe.matmul(T.ps3[:, 0:C], T.ID[:], T.PROD[:, C * x:C * x + C], x == 0, x == N - 1))
+    summed = n["t"]
+    vw()
+    for i in range(3):
+        v(ve.tensor_scalar(T.MR[:, N * C + W3 * i:N * C + W3 * i + W3], T.PROD[:, W3 * i:W3 * i + W3], 128.0, None, Op.is_ge))
+    ve.wait_ge(T.sem.t, summed)
+    v(ve.tensor_scalar(T.T1[:], T.ps3[:, 0:C], 128.0, -128.0, Op.is_ge, Op.mult))
+    vw()
+    v(ve.tensor_tensor(T.ROW[:], T.T1[:], T.ps3[:, 0:C], Op.add))
+    vw()
+    for c in range(C):
+        w = 32 * (c // 16) + this + c % 16
+        hot = T.HOT[:, 128 * c:128 * c + 128]
+        v(ve.tensor_scalar(hot, T.IOH[:], T.ROW[:, c:c + 1], T.VAL[:, w:w + 1], Op.is_equal, Op.mult))
+        pe.wait_ge(T.sem.v, n["v"])
+        t(pe.matmul(T.ps4[:, 0:24], hot, T.MR[:, c:2 * N * C:C], c == 0, c == C - 1))
+    filled = n["t"]
+    out = T.OA if kind == "X" else T.OB
+    if kind == "P":
+        v(ve.tensor_scalar(T.DF[:], T.ps6[:, 0:C], float(S * N), None, Op.add))
+        vw()
+        v(ve.tensor_tensor(T.DG[:], T.DF[:], T.ps3[:, 0:C], Op.add))
+        vw()
+        v(ve.tensor_copy(T.OB[:, 192:288], T.DG[:]))
+    ve.wait_ge(T.sem.t, filled)
+    v(ve.tensor_copy(T.PF[:, 1:24:2], T.ps4[:, 12:24]))
+    vw()
+    v(ve.tensor_tensor(T.PF[:, 0:24:2], T.ps4[:, 0:12], T.PF[:, 1:24:2], Op.subtract))
+    pe.wait_ge(T.sem.v, n["v"])
+    for k in range(8):
+        t(pe.matmul(T.ps5[:, k:192:8], T.WK[:, 128 * k:128 * k + 128], T.PF[:], True, True))
+    ve.wait_ge(T.sem.t, n["t"])
+    listed = v(ve.tensor_scalar(out[:, 0:192], T.ps5[:, 0:192], 2048.0, None, Op.add))
+
+    if kind == "P":
+        at = 0
+        for k, ds in enumerate(HELPED):
+            g.wait_ge(T.sem["fw%d" % k], len(inner))
+            parts = split(off_chip, len(ds))
+            g.remote_dma_fused([RemoteDMATransfer(src=T.FWD[:, S * (at + m):S * (at + m + 1)], dst=T.RECV[:, S * r:S * r + S],
+                                                  dst_ids=[dst(X[(r + d) % N])], dma_engine_mask=mask_of(parts[m]),
+                                                  remote_sem=T.sem["col%d" % r]) for m, d in enumerate(ds)], local_sem=T.sem.ls)
+            n["ls"] += sum(len(p) for p in parts)
+            at += len(ds)
+        g.wait_ge(T.sem.v, n["v"])
+        write(T.OB[:], T.OB[:], X[r], "ob", off_chip)
+        g.wait_ge(T.sem.ls, n["ls"])
+        return
+
+    ve.wait_ge(T.sem.lta, 16)
+    ve.wait_ge(T.sem.v, listed)
+    sc.wait_ge(T.sem.lta, 16)
+    sc.wait_ge(T.sem.v, listed)
+    helped = [d for ds in HELPED for d in ds]
+    straight = [d for ds in STRAIGHT for d in ds]
+    got = {}
+    for k, d in enumerate(helped):
+        b = (r + d) % N
+        got[d] = v(ve.tensor_copy(T.COL[:, S * k:S * k + S], T.TAS[:, 0:4096].indirect(T.OA[:, 16 * b:16 * b + 16])))
+    for k, d in enumerate(straight):
+        b, at = (r + d) % N, len(helped) + k
+        got[d] = a(sc.activation(T.COL[:, S * at:S * at + S], T.TAS[:, 0:4096].indirect(T.OA[:, 16 * b:16 * b + 16]), Fn.Copy))
+    own = a(sc.activation(T.RECV[:, S * r:S * r + S], T.TAS[:, 0:4096].indirect(T.OA[:, 16 * r:16 * r + 16]), Fn.Copy))
+    at, to = 0, len(helped)
+    for k in range(2):
+        g.wait_ge(T.sem.v, got[HELPED[k][-1]])
+        w = len(HELPED[k])
+        write(T.FWD[:, S * at:S * (at + w)], T.COL[:, S * at:S * (at + w)], P[r], "fw%d" % k, inner)
+        at += w
+        g.wait_ge(T.sem.a, got[STRAIGHT[k][-1]])
+        parts = split(off_chip, len(STRAIGHT[k]))
+        g.remote_dma_fused([RemoteDMATransfer(src=T.COL[:, S * (to + m):S * (to + m + 1)], dst=T.RECV[:, S * r:S * r + S],
+                                              dst_ids=[dst(X[(r + d) % N])], dma_engine_mask=mask_of(parts[m]),
+                                              remote_sem=T.sem["col%d" % r]) for m, d in enumerate(STRAIGHT[k])], local_sem=T.sem.ls)
+        n["ls"] += sum(len(p) for p in parts)
+        to += len(STRAIGHT[k])
+
+    ve.wait_ge(T.sem.ltb, 16)
+    ve.wait_ge(T.sem.ob, len(off_chip))
+    banks = [T.ps0, T.ps1, T.ps2, T.ps3, T.ps4, T.ps5, T.ps6, T.ps7]
+    turn = [(0, 0)]
+    for ds in (STRAIGHT[0], HELPED[0], STRAIGHT[1], HELPED[1]):
+        turn += [(d, len(p)) for d, p in zip(ds, split(off_chip, len(ds)))]
+    copied = []
+    for k, (d, e) in enumerate(turn):
+        s = (r - d) % N
+        if d == 0:
+            ve.wait_ge(T.sem.a, own)
+        else:
+            ve.wait_ge(T.sem["col%d" % s], e)
+        blk = T.PR[:, S * s:S * s + S]
+        pe.wait_ge(T.sem.v, v(ve.tensor_tensor(blk, T.TBS[:, 0:4096].indirect(T.OB[:, 16 * s:16 * s + 16]), T.RECV[:, S * s:S * s + S], Op.mult)))
+        if k >= 8:
+            pe.wait_ge(T.sem.a, copied[k - 8])
+        sc.wait_ge(T.sem.t, t(pe.matmul(banks[k % 8][:, 0:S], T.ONE32[:], blk, True, True)))
+        copied.append(a(sc.activation(T.WIN[:, S * s:S * s + S], banks[k % 8][:, 0:S], Fn.Copy)))
+    ve.wait_ge(T.sem.a, n["a"])
+    sc.wait_ge(T.sem.a, n["a"])
+    sc.wait_ge(T.sem.ob, len(off_chip))
+    done = []
+    for j in range(BLK):
+        o, w = T.D[:, 512 * j:512 * j + 512], T.WIN[:, 0:N * S + 8].indirect(T.OB[:, 192 + 32 * j:224 + 32 * j])
+        done.append((T.sem.a, a(sc.activation(o, w, Fn.Copy))) if j == 1 else (T.sem.v, v(ve.tensor_copy(o, w))))
+
+    for j in range(BLK):
+        sy.wait_ge(done[j][0], done[j][1])
+        sy.dma_start(T.RET[4 * j:4 * j + 4], T.D[0:128:16, 512 * j:512 * j + 512]).then_inc(T.sem["rd%d" % j], 16)
+        parts = split(off_chip, 4)
+        g.wait_ge(T.sem["rd%d" % j], 16)
+        tr = []
+        for q in range(4 * j, 4 * j + 4):
+            if q == r:
+                continue
+            tr.append(RemoteDMATransfer(src=T.RET[q], dst=T.BACK[r], dst_ids=[dst(X[q])], dma_engine_mask=mask_of(parts[q % 4]),
+                                        remote_sem=T.sem.back))
+            n["ls"] += len(parts[q % 4])
+        g.remote_dma_fused(tr, local_sem=T.sem.ls)
+    j, p0 = r // 4, 32 * (r % 4)
+    sc.wait_ge(done[j][0], done[j][1])
+    sc.dma_start(T.BACK[r], T.D[p0:p0 + 32:16, 512 * j:512 * j + 512]).then_inc(T.sem.bk, 16)
+    sy.wait_ge(T.sem.bk, 16)
+    sy.wait_ge(T.sem.back, (N - 1) * len(off_chip) // 4)
+    sy.dma_start(T.FIN[:], T.BACK[:]).then_inc(T.sem.fin, 16)
+    pe.wait_ge(T.sem.fin, 16)
+    pe.wait_ge(T.sem.a, copied[8])
+    for m in range(16):
+        t(pe.matmul(T.ps0[0:32, 0:32], T.Z[0:24, 15 - m:47 - m], T.FIN[0:24, m:512:16], m == 0, m == 15))
+    ve.wait_ge(T.sem.t, n["t"])
+    v(ve.tensor_copy(T.Y[:], T.ps0[0:32, 0:32]))
+    sy.wait_ge(T.sem.v, n["v"])
+    sy.dma_start(T.y[:], T.Y[:]).then_inc(T.sem.st, 16)
+    sy.wait_ge(T.sem.st, 16)
+    g.wait_ge(T.sem.ls, n["ls"])

@@ -1,4 +1,5 @@
 from concourse.bass import DstId, RemoteDMATransfer
+from concourse.mybir import AxisListType
 from concourse.mybir import AluOpType as Op
 from concourse.mybir import ActivationFunctionType as Fn
 
@@ -7,8 +8,9 @@ C = 96
 S = 256
 BLK = 3
 WORLD = 256
-STRAIGHT = ((2, 10), (4, 8, 1, 11))
-HELPED = ((3, 9), (5, 7, 6))
+STRAIGHT = ((2, 10), (4, 8), (1, 11))
+HELPED = ((3,), (9, 5), (7, 6))
+CALLS = ((0, 1, 2, 3, 4, 5, 6, 7), (8, 9, 10, 11))
 
 SCRATCH = {
     "LAND": ("dram", [N, 128, 16], "int32"),
@@ -30,16 +32,15 @@ SCRATCH = {
     "HOT": ("sbuf", [128, C * 128], "float16"),
     "PF": ("sbuf", [128, 24], "float16"),
     "OA": ("sbuf", [128, 192], "uint16"),
-    "OB": ("sbuf", [128, 288], "uint16"),
-    "DF": ("sbuf", [128, C], "float32"),
-    "DG": ("sbuf", [128, C], "float32"),
+    "OB": ("sbuf", [128, 192], "uint16"),
+    "OD": ("sbuf", [128, C], "uint16"),
     "COL": ("sbuf", [128, 11 * S], "float32"),
     "FWD": ("sbuf", [128, 5 * S], "float32"),
     "RECV": ("sbuf", [128, N * S], "float32"),
     "PR": ("sbuf", [128, N * S], "float32"),
     "WIN": ("sbuf", [128, N * S + 8], "float32"),
     "D": ("sbuf", [128, 16 * C], "float32"),
-    "FIN": ("sbuf", [24, 512], "float32"),
+    "FIN": ("sbuf", [96, 516], "float32"),
     "Y": ("sbuf", [32, 32], "float32"),
     "IOF": ("sbuf", [128, 128], "float32"),
     "IOH": ("sbuf", [128, 128], "float16"),
@@ -50,6 +51,7 @@ SCRATCH = {
     "PI1": ("sbuf", [128, 1], "int32"),
     "PI2": ("sbuf", [128, 1], "int32"),
     "PF2": ("sbuf", [128, 1], "float32"),
+    "GE": ("sbuf", [128, 4], "float32"),
     "TM": ("sbuf", [128, 128], "float16"),
     "ONEH": ("sbuf", [128, 128], "float16"),
     "ID": ("sbuf", [128, 128], "float16"),
@@ -61,7 +63,7 @@ SCRATCH = {
 for _i in range(8):
     SCRATCH["ps%d" % _i] = ("psum", [128, 512], "float32")
 
-SEMAPHORES = (["v", "t", "a", "gi", "own", "lst", "lsx", "ld", "lta", "ltb", "ob", "ls", "bk", "back", "fin", "st"]
+SEMAPHORES = (["v", "t", "a", "gi", "own", "lst", "ld", "lta", "ltb", "ob", "od", "ls", "bk", "back", "fin", "st"]
               + ["rd%d" % j for j in range(BLK)] + ["fw%d" % k for k in range(len(HELPED))] + ["col%d" % a for a in range(N)])
 
 
@@ -86,17 +88,9 @@ def helper(x, cores, topo):
             return c
 
 
-def shares(n):
-    return {1: (1,), 2: (2, 2), 3: (2, 4, 4), 4: (4, 4, 4, 4)}[n]
-
-
 def split(engines, n):
-    out, at = [], 0
-    for s in shares(n):
-        k = len(engines) // s
-        out.append(engines[at:at + k])
-        at += k
-    return out
+    w = len(engines) // n
+    return [engines[w * k:w * k + w] for k in range(n)]
 
 
 def rank_program(g, core, T, topo):
@@ -147,10 +141,10 @@ def rank_program(g, core, T, topo):
         g.remote_dma(out, src, T.sem[sem], T.sem.ls, pid, rid, mask_of(engines))
         n["ls"] += len(engines)
 
-    def cast(src, dests, out, sem, engines):
-        g.remote_dma_fused([RemoteDMATransfer(src=src, dsts=[out for d in dests], dst_ids=[dst(d) for d in dests],
-                                              dma_engine_mask=mask_of(engines), remote_sem=T.sem[sem])], local_sem=T.sem.ls)
-        n["ls"] += len(engines)
+    def cast(groups):
+        g.remote_dma_fused([RemoteDMATransfer(src=T.LAND[r], dsts=[T.LAND[r] for d in ds], dst_ids=[dst(d) for d in ds],
+                                              dma_engine_mask=mask_of(es), remote_sem=T.sem.lst) for ds, es in groups], local_sem=T.sem.ls)
+        n["ls"] += sum(len(es) for ds, es in groups)
 
     if kind == "X":
         sy.dma_start(T.LAND[r, 0:128:2, :], T.pi[:]).then_inc(T.sem.own, 16)
@@ -162,17 +156,13 @@ def rank_program(g, core, T, topo):
     g.iota(T.PI1[:], [[0, 1]], 0, 1).then_inc(T.sem.gi, 1)
     if kind == "X":
         g.wait_ge(T.sem.own, 32)
-        cast(T.LAND[r], [x for x in X if x != core], T.LAND[r], "lst", off_chip)
-        write(T.LAND[r], T.LAND[r], P[r], "lsx", inner)
-        mine, count = "own", 32
-    else:
-        g.wait_ge(T.sem.lsx, len(inner))
-        cast(T.LAND[r], [p for p in P if p != core], T.LAND[r], "lst", off_chip)
-        mine, count = "lsx", len(inner)
+        cast([([x for x in X if x != core], off_chip)])
+        cast([([p for p in P if p != P[r]], off_chip), ([P[r]], inner)])
     g.iota(T.SEGF[:], [[0, 4], [1, C]], 0, 0, **F).then_inc(T.sem.gi, 1)
     for q in (sy, sc):
-        q.wait_ge(T.sem[mine], count)
-        q.wait_ge(T.sem.lst, (N - 1) * len(off_chip))
+        if kind == "X":
+            q.wait_ge(T.sem.own, 32)
+        q.wait_ge(T.sem.lst, (N - 1) * len(off_chip) + (len(inner) if kind == "P" else 0))
     for j in range(BLK):
         (sy, sc, sy)[j].dma_start(T.L[:, 64 * j:64 * j + 64], T.LAND[4 * j:4 * j + 4]).then_inc(T.sem.ld, 16)
     if kind == "X":
@@ -192,11 +182,6 @@ def rank_program(g, core, T, topo):
     if kind == "X":
         v(ve.memset(T.ONE32[:], 1.0))
         v(ve.memset(T.WIN[:, N * S:N * S + 8], 0.0))
-        v(ve.tensor_scalar(T.PI2[:], T.PI1[:], 1, None, Op.bitwise_and))
-        vw()
-        v(ve.tensor_scalar(T.PF2[:], T.PI2[:], 16.0, 15.0, Op.mult, Op.add))
-        vw()
-        v(ve.tensor_scalar(T.Z[:], T.IOF[:, 0:48], T.PF2[:, 0:1], None, Op.is_equal))
     else:
         for x in range(N):
             v(ve.tensor_scalar(T.IDX[:, 128 * x:128 * x + 128], T.IOF[:], part, float(S * x - S * N), Op.is_equal, Op.mult))
@@ -237,12 +222,16 @@ def rank_program(g, core, T, topo):
         chosen.append(v(ve.tensor_tensor(T.PROD[:, W3 * i:W3 * i + W3], T.MR[:, W3 * i:W3 * i + W3], pos[i][:, 0:W3], Op.mult)))
     if kind == "P":
         for x in range(N):
-            t(pe.matmul(T.ps6[:, 0:C], T.IDX[:, 128 * x:128 * x + 128], T.MR[:, C * x:C * x + C], x == 0, x == N - 1))
+            t(pe.matmul(T.ps6[:, 0:C], T.IDX[:, 128 * x:128 * x + 128], T.MR[:, C * x:C * x + C], x == 0, False))
     for x in range(N):
         if x % 4 == 0:
             pe.wait_ge(T.sem.v, chosen[x // 4])
         t(pe.matmul(T.ps3[:, 0:C], T.ID[:], T.PROD[:, C * x:C * x + C], x == 0, x == N - 1))
     summed = n["t"]
+    if kind == "P":
+        for x in range(N):
+            t(pe.matmul(T.ps6[:, 0:C], T.ID[:], T.PROD[:, C * x:C * x + C], False, x == N - 1))
+    windowed = n["t"]
     vw()
     for i in range(3):
         v(ve.tensor_scalar(T.MR[:, N * C + W3 * i:N * C + W3 * i + W3], T.PROD[:, W3 * i:W3 * i + W3], 128.0, None, Op.is_ge))
@@ -252,20 +241,17 @@ def rank_program(g, core, T, topo):
     v(ve.tensor_tensor(T.ROW[:], T.T1[:], T.ps3[:, 0:C], Op.add))
     vw()
     for c in range(C):
+        if kind == "P" and c == 24:
+            ve.wait_ge(T.sem.t, windowed)
+            g.wait_ge(T.sem.v, v(ve.tensor_scalar(T.OD[:], T.ps6[:, 0:C], float(S * N), None, Op.add)))
+            write(T.OD[:], T.OD[:], X[r], "od", off_chip)
         w = 32 * (c // 16) + this + c % 16
         hot = T.HOT[:, 128 * c:128 * c + 128]
         v(ve.tensor_scalar(hot, T.IOH[:], T.ROW[:, c:c + 1], T.VAL[:, w:w + 1], Op.is_equal, Op.mult))
         pe.wait_ge(T.sem.v, n["v"])
         t(pe.matmul(T.ps4[:, 0:24], hot, T.MR[:, c:2 * N * C:C], c == 0, c == C - 1))
-    filled = n["t"]
     out = T.OA if kind == "X" else T.OB
-    if kind == "P":
-        v(ve.tensor_scalar(T.DF[:], T.ps6[:, 0:C], float(S * N), None, Op.add))
-        vw()
-        v(ve.tensor_tensor(T.DG[:], T.DF[:], T.ps3[:, 0:C], Op.add))
-        vw()
-        v(ve.tensor_copy(T.OB[:, 192:288], T.DG[:]))
-    ve.wait_ge(T.sem.t, filled)
+    ve.wait_ge(T.sem.t, n["t"])
     v(ve.tensor_copy(T.PF[:, 1:24:2], T.ps4[:, 12:24]))
     vw()
     v(ve.tensor_tensor(T.PF[:, 0:24:2], T.ps4[:, 0:12], T.PF[:, 1:24:2], Op.subtract))
@@ -273,20 +259,17 @@ def rank_program(g, core, T, topo):
     for k in range(8):
         t(pe.matmul(T.ps5[:, k:192:8], T.WK[:, 128 * k:128 * k + 128], T.PF[:], True, True))
     ve.wait_ge(T.sem.t, n["t"])
-    listed = v(ve.tensor_scalar(out[:, 0:192], T.ps5[:, 0:192], 2048.0, None, Op.add))
+    listed = v(ve.tensor_scalar(out[:], T.ps5[:, 0:192], 2048.0, None, Op.add))
 
     if kind == "P":
+        g.wait_ge(T.sem.v, listed)
+        write(T.OB[:], T.OB[:], X[r], "ob", off_chip)
         at = 0
         for k, ds in enumerate(HELPED):
             g.wait_ge(T.sem["fw%d" % k], len(inner))
-            parts = split(off_chip, len(ds))
-            g.remote_dma_fused([RemoteDMATransfer(src=T.FWD[:, S * (at + m):S * (at + m + 1)], dst=T.RECV[:, S * r:S * r + S],
-                                                  dst_ids=[dst(X[(r + d) % N])], dma_engine_mask=mask_of(parts[m]),
-                                                  remote_sem=T.sem["col%d" % r]) for m, d in enumerate(ds)], local_sem=T.sem.ls)
-            n["ls"] += sum(len(p) for p in parts)
-            at += len(ds)
-        g.wait_ge(T.sem.v, n["v"])
-        write(T.OB[:], T.OB[:], X[r], "ob", off_chip)
+            for d in ds:
+                write(T.RECV[:, S * r:S * r + S], T.FWD[:, S * at:S * at + S], X[(r + d) % N], "col%d" % r, off_chip)
+                at += 1
         g.wait_ge(T.sem.ls, n["ls"])
         return
 
@@ -305,7 +288,7 @@ def rank_program(g, core, T, topo):
         got[d] = a(sc.activation(T.COL[:, S * at:S * at + S], T.TAS[:, 0:4096].indirect(T.OA[:, 16 * b:16 * b + 16]), Fn.Copy))
     own = a(sc.activation(T.RECV[:, S * r:S * r + S], T.TAS[:, 0:4096].indirect(T.OA[:, 16 * r:16 * r + 16]), Fn.Copy))
     at, to = 0, len(helped)
-    for k in range(2):
+    for k in range(len(HELPED)):
         g.wait_ge(T.sem.v, got[HELPED[k][-1]])
         w = len(HELPED[k])
         write(T.FWD[:, S * at:S * (at + w)], T.COL[:, S * at:S * (at + w)], P[r], "fw%d" % k, inner)
@@ -318,12 +301,21 @@ def rank_program(g, core, T, topo):
         n["ls"] += sum(len(p) for p in parts)
         to += len(STRAIGHT[k])
 
+    v(ve.tensor_scalar(T.PI2[:], T.PI1[:], 1, None, Op.bitwise_and))
+    for f in range(1, 4):
+        v(ve.tensor_scalar(T.GE[:, f:f + 1], part, 24.0 * f, None, Op.is_ge))
+    vw()
+    v(ve.tensor_scalar(T.PF2[:], T.PI2[:], 16.0, 12.0, Op.mult, Op.add))
+    v(ve.tensor_reduce(T.GE[:, 0:1], T.GE[:, 1:4], AxisListType.X, Op.add))
+    vw()
+    v(ve.tensor_scalar(T.Z[:], T.IOF[:, 0:48], T.PF2[:, 0:1], T.GE[:, 0:1], Op.subtract, Op.is_equal))
+
     ve.wait_ge(T.sem.ltb, 16)
     ve.wait_ge(T.sem.ob, len(off_chip))
     banks = [T.ps0, T.ps1, T.ps2, T.ps3, T.ps4, T.ps5, T.ps6, T.ps7]
     turn = [(0, 0)]
-    for ds in (STRAIGHT[0], HELPED[0], STRAIGHT[1], HELPED[1]):
-        turn += [(d, len(p)) for d, p in zip(ds, split(off_chip, len(ds)))]
+    for k in range(len(HELPED)):
+        turn += [(d, len(off_chip) // len(STRAIGHT[k])) for d in STRAIGHT[k]] + [(d, len(off_chip)) for d in HELPED[k]]
     copied = []
     for k, (d, e) in enumerate(turn):
         s = (r - d) % N
@@ -337,37 +329,44 @@ def rank_program(g, core, T, topo):
             pe.wait_ge(T.sem.a, copied[k - 8])
         sc.wait_ge(T.sem.t, t(pe.matmul(banks[k % 8][:, 0:S], T.ONE32[:], blk, True, True)))
         copied.append(a(sc.activation(T.WIN[:, S * s:S * s + S], banks[k % 8][:, 0:S], Fn.Copy)))
-    ve.wait_ge(T.sem.a, n["a"])
-    sc.wait_ge(T.sem.a, n["a"])
-    sc.wait_ge(T.sem.ob, len(off_chip))
-    done = []
-    for j in range(BLK):
-        o, w = T.D[:, 512 * j:512 * j + 512], T.WIN[:, 0:N * S + 8].indirect(T.OB[:, 192 + 32 * j:224 + 32 * j])
-        done.append((T.sem.a, a(sc.activation(o, w, Fn.Copy))) if j == 1 else (T.sem.v, v(ve.tensor_copy(o, w))))
+    for q in (ve, sc):
+        q.wait_ge(T.sem.a, n["a"])
+        q.wait_ge(T.sem.od, len(off_chip))
+
+    def spread(engine, c0, c1):
+        o, w = T.D[:, 16 * c0:16 * c1], T.WIN[:, 0:N * S + 8].indirect(T.OD[:, c0:c1])
+        return v(ve.tensor_copy(o, w)) if engine == "v" else a(sc.activation(o, w, Fn.Copy))
+
+    done = [{"v": spread("v", 0, 32)}, {"a": spread("a", 32, 64)}, {"v": spread("v", 64, 80), "a": spread("a", 80, 96)}]
+
+    def after(queue, j):
+        for name in done[j]:
+            queue.wait_ge(T.sem[name], done[j][name])
 
     for j in range(BLK):
-        sy.wait_ge(done[j][0], done[j][1])
+        after(sy, j)
         sy.dma_start(T.RET[4 * j:4 * j + 4], T.D[0:128:16, 512 * j:512 * j + 512]).then_inc(T.sem["rd%d" % j], 16)
-        parts = split(off_chip, 4)
-        g.wait_ge(T.sem["rd%d" % j], 16)
-        tr = []
-        for q in range(4 * j, 4 * j + 4):
-            if q == r:
-                continue
-            tr.append(RemoteDMATransfer(src=T.RET[q], dst=T.BACK[r], dst_ids=[dst(X[q])], dma_engine_mask=mask_of(parts[q % 4]),
-                                        remote_sem=T.sem.back))
-            n["ls"] += len(parts[q % 4])
+    for qs in CALLS:
+        for j in sorted({q // 4 for q in qs}):
+            g.wait_ge(T.sem["rd%d" % j], 16)
+        w = len(off_chip) // len(qs)
+        tr = [RemoteDMATransfer(src=T.RET[q], dst=T.BACK[r], dst_ids=[dst(X[q])], remote_sem=T.sem.back,
+                                dma_engine_mask=mask_of(off_chip[w * k:w * k + w])) for k, q in enumerate(qs) if q != r]
         g.remote_dma_fused(tr, local_sem=T.sem.ls)
+        n["ls"] += w * len(tr)
     j, p0 = r // 4, 32 * (r % 4)
-    sc.wait_ge(done[j][0], done[j][1])
+    after(sc, j)
     sc.dma_start(T.BACK[r], T.D[p0:p0 + 32:16, 512 * j:512 * j + 512]).then_inc(T.sem.bk, 16)
-    sy.wait_ge(T.sem.bk, 16)
-    sy.wait_ge(T.sem.back, (N - 1) * len(off_chip) // 4)
-    sy.dma_start(T.FIN[:], T.BACK[:]).then_inc(T.sem.fin, 16)
-    pe.wait_ge(T.sem.fin, 16)
+    w = next(len(off_chip) // len(qs) for qs in CALLS if r in qs)
+    for q in (sy, sc):
+        q.wait_ge(T.sem.bk, 16)
+        q.wait_ge(T.sem.back, (N - 1) * w)
+    for f in range(4):
+        (sy, sc)[f % 2].dma_start(T.FIN[24 * f:24 * f + 24, 3 - f:515 - f], T.BACK[:]).then_inc(T.sem.fin, 16)
+    pe.wait_ge(T.sem.fin, 64)
     pe.wait_ge(T.sem.a, copied[8])
-    for m in range(16):
-        t(pe.matmul(T.ps0[0:32, 0:32], T.Z[0:24, 15 - m:47 - m], T.FIN[0:24, m:512:16], m == 0, m == 15))
+    for k in range(4):
+        t(pe.matmul(T.ps0[0:32, 0:32], T.Z[0:96, 12 - 4 * k:44 - 4 * k], T.FIN[0:96, 3 + 4 * k:512:16], k == 0, k == 3))
     ve.wait_ge(T.sem.t, n["t"])
     v(ve.tensor_copy(T.Y[:], T.ps0[0:32, 0:32]))
     sy.wait_ge(T.sem.v, n["v"])

@@ -7,10 +7,12 @@ N = 12
 C = 96
 S = 256
 BLK = 3
+HEAD = 2
 WORLD = 256
 STRAIGHT = ((2, 10), (4, 8), (1, 11))
 HELPED = ((3,), (9, 5), (7, 6))
 CALLS = ((0, 1, 2, 3, 4, 5, 6, 7), (8, 9, 10, 11))
+EARLY = 1280
 
 SCRATCH = {
     "LAND": ("dram", [N, 128, 16], "int32"),
@@ -18,19 +20,23 @@ SCRATCH = {
     "BACK": ("dram", [N, 128, 8], "float32"),
     "TAS": ("sbuf", [128, 4096], "float32"),
     "TBS": ("sbuf", [128, 4096], "float32"),
-    "L": ("sbuf", [128, 192], "int32"),
-    "HG": ("sbuf", [128, 192], "int32"),
-    "UV": ("sbuf", [128, 192], "int32"),
-    "VAL": ("sbuf", [128, 192], "float32"),
-    "NOT": ("sbuf", [128, 192], "float16"),
+    "L": ("sbuf", [128, 128], "int32"),
+    "HG": ("sbuf", [128, 128], "int32"),
+    "UV": ("sbuf", [128, 128], "int32"),
+    "VAL": ("sbuf", [128, 128], "float32"),
+    "NOT": ("sbuf", [128, 128], "float16"),
     "KEY": ("sbuf", [128, C], "float16"),
     "MR": ("sbuf", [128, 2 * N * C], "float16"),
     "SC": ("sbuf", [128, N * C], "float16"),
     "PROD": ("sbuf", [128, N * C], "float16"),
     "T1": ("sbuf", [128, C], "float32"),
     "ROW": ("sbuf", [128, C], "float32"),
-    "HOT": ("sbuf", [128, C * 128], "float16"),
+    "HOT": ("sbuf", [128, 64 * 128], "float16"),
     "PF": ("sbuf", [128, 24], "float16"),
+    "PG": ("sbuf", [128, 24], "float16"),
+    "PT0": ("sbuf", [128, 24], "float16"),
+    "PT1": ("sbuf", [128, 24], "float16"),
+    "PS": ("sbuf", [128, 24], "float16"),
     "OA": ("sbuf", [128, 192], "uint16"),
     "OB": ("sbuf", [128, 192], "uint16"),
     "OD": ("sbuf", [128, C], "uint16"),
@@ -46,8 +52,8 @@ SCRATCH = {
     "IOH": ("sbuf", [128, 128], "float16"),
     "PK": ("sbuf", [128, 8], "float32"),
     "MODF": ("sbuf", [128, 128], "float32"),
-    "SEGF": ("sbuf", [128, 4 * C], "float32"),
-    "SEG": ("sbuf", [128, 4 * C], "float16"),
+    "SEGF": ("sbuf", [128, 256], "float32"),
+    "SEG": ("sbuf", [128, 256], "float16"),
     "PI1": ("sbuf", [128, 1], "int32"),
     "PI2": ("sbuf", [128, 1], "int32"),
     "PF2": ("sbuf", [128, 1], "float32"),
@@ -55,6 +61,7 @@ SCRATCH = {
     "TM": ("sbuf", [128, 128], "float16"),
     "ONEH": ("sbuf", [128, 128], "float16"),
     "ID": ("sbuf", [128, 128], "float16"),
+    "NID": ("sbuf", [128, 128], "float16"),
     "WK": ("sbuf", [128, 8 * 128], "float16"),
     "IDX": ("sbuf", [128, N * 128], "float16"),
     "ONE32": ("sbuf", [128, 128], "float32"),
@@ -63,7 +70,7 @@ SCRATCH = {
 for _i in range(8):
     SCRATCH["ps%d" % _i] = ("psum", [128, 512], "float32")
 
-SEMAPHORES = (["v", "t", "a", "gi", "own", "lst", "ld", "lta", "ltb", "ob", "od", "ls", "bk", "back", "fin", "st"]
+SEMAPHORES = (["v", "t", "a", "gi", "own", "lst", "ld", "lta", "ltb", "ob", "od", "pt0", "pt1", "ls", "bk", "back", "fin", "st"]
               + ["rd%d" % j for j in range(BLK)] + ["fw%d" % k for k in range(len(HELPED))] + ["col%d" % a for a in range(N)])
 
 
@@ -88,29 +95,39 @@ def helper(x, cores, topo):
             return c
 
 
+def beside(x, topo):
+    for c in range(WORLD):
+        if c != x and same_chip(c, x, topo) and topo.die(c) == topo.die(x):
+            return c
+
+
 def split(engines, n):
     w = len(engines) // n
     return [engines[w * k:w * k + w] for k in range(n)]
 
 
 def rank_program(g, core, T, topo):
-    cores = list(T.cores)
-    me = None
-    for q, x in enumerate(cores):
+    X = list(T.cores)
+    r = None
+    for q, x in enumerate(X):
         if same_chip(core, x, topo):
-            if core == x:
-                me = ("X", q)
-            elif core == helper(x, cores, topo):
-                me = ("P", q)
-    if me is None:
+            r = q
+    if r is None:
         return
-    kind, r = me
-    X = cores
-    P = [helper(x, cores, topo) for x in cores]
-    far = next(x for x in X if not same_chip(x, core, topo))
+    P = [helper(x, X, topo) for x in X]
+    Z = [beside(x, topo) for x in X]
+    W = [beside(p, topo) for p in P]
+    kind = None
+    for name, group in (("X", X), ("P", P), ("Z", Z), ("W", W)):
+        if core == group[r]:
+            kind = name
+    if kind is None:
+        return
+    head = kind in ("X", "P")
+    far = next(x for x in X if topo.may_write(core, x) and not same_chip(x, core, topo))
     off_chip = bits(topo.mask(core, far))
-    on_chip = bits(topo.mask(core, P[r] if kind == "X" else X[r]))
-    inner = [e for e in on_chip if e not in off_chip]
+    near = {"X": P, "P": X, "Z": X, "W": P}[kind][r]
+    inner = [e for e in bits(topo.mask(core, near)) if e not in off_chip]
     ve, pe, sc, sy = g.vector, g.tensor, g.scalar, g.sync
     n = {"v": 0, "t": 0, "a": 0, "ls": 0}
 
@@ -141,14 +158,24 @@ def rank_program(g, core, T, topo):
         g.remote_dma(out, src, T.sem[sem], T.sem.ls, pid, rid, mask_of(engines))
         n["ls"] += len(engines)
 
-    def cast(groups):
-        g.remote_dma_fused([RemoteDMATransfer(src=T.LAND[r], dsts=[T.LAND[r] for d in ds], dst_ids=[dst(d) for d in ds],
-                                              dma_engine_mask=mask_of(es), remote_sem=T.sem.lst) for ds, es in groups], local_sem=T.sem.ls)
-        n["ls"] += sum(len(es) for ds, es in groups)
+    def cast(group):
+        tr = []
+        for ds, es in (([d for d in group if not same_chip(d, core, topo)], off_chip),
+                       ([d for d in group if same_chip(d, core, topo) and d != core], inner)):
+            if ds:
+                tr.append(RemoteDMATransfer(src=T.LAND[r], dsts=[T.LAND[r] for d in ds], dst_ids=[dst(d) for d in ds],
+                                            dma_engine_mask=mask_of(es), remote_sem=T.sem.lst))
+                n["ls"] += len(es)
+        g.remote_dma_fused(tr, local_sem=T.sem.ls)
 
+    mine = list(range(HEAD)) if head else list(range(HEAD, BLK))
+    CC = 32 * len(mine)
+    lists = [4 * j + k for j in mine for k in range(4)]
+    ours = kind == "X" and r in lists
     if kind == "X":
         sy.dma_start(T.LAND[r, 0:128:2, :], T.pi[:]).then_inc(T.sem.own, 16)
         sc.dma_start(T.LAND[r, 1:128:2, :], T.pj[:]).then_inc(T.sem.own, 16)
+        sy.dma_start(T.TAS[:, 0:EARLY], T.ta[:, 0:EARLY]).then_inc(T.sem.lta, 16)
     F = {"allow_small_or_imprecise_dtypes": True}
     g.iota(T.IOF[:], [[1, 128]], 0, 0, **F).then_inc(T.sem.gi, 1)
     g.iota(T.PK[:], [[-16, 8]], 0, 1, **F).then_inc(T.sem.gi, 1)
@@ -156,108 +183,137 @@ def rank_program(g, core, T, topo):
     g.iota(T.PI1[:], [[0, 1]], 0, 1).then_inc(T.sem.gi, 1)
     if kind == "X":
         g.wait_ge(T.sem.own, 32)
-        cast([([x for x in X if x != core], off_chip)])
-        cast([([p for p in P if p != P[r]], off_chip), ([P[r]], inner)])
-    g.iota(T.SEGF[:], [[0, 4], [1, C]], 0, 0, **F).then_inc(T.sem.gi, 1)
-    for q in (sy, sc):
-        if kind == "X":
-            q.wait_ge(T.sem.own, 32)
-        q.wait_ge(T.sem.lst, (N - 1) * len(off_chip) + (len(inner) if kind == "P" else 0))
-    for j in range(BLK):
-        (sy, sc, sy)[j].dma_start(T.L[:, 64 * j:64 * j + 64], T.LAND[4 * j:4 * j + 4]).then_inc(T.sem.ld, 16)
+        for group in ((X, P) if r < 4 * HEAD else (Z, W)):
+            cast(group)
+    g.iota(T.SEGF[:, 0:4 * CC], [[0, 4], [1, CC]], 0, 0, **F).then_inc(T.sem.gi, 1)
+    if ours:
+        sy.wait_ge(T.sem.own, 32)
+    sy.wait_ge(T.sem.lst, sum(len(inner) if same_chip(X[q], core, topo) else len(off_chip) for q in lists if not (ours and q == r)))
+    for k, j in enumerate(mine):
+        sy.dma_start(T.L[:, 64 * k:64 * k + 64], T.LAND[4 * j:4 * j + 4]).then_inc(T.sem.ld, 16)
     if kind == "X":
-        sy.wait_ge(T.sem.ld, 16 * BLK)
-        sy.dma_start(T.TAS[:], T.ta[:]).then_inc(T.sem.lta, 16)
+        sy.dma_start(T.TAS[:, EARLY:4096], T.ta[:, EARLY:4096]).then_inc(T.sem.lta, 16)
         sy.dma_start(T.TBS[:], T.tb[:]).then_inc(T.sem.ltb, 16)
 
     ve.wait_ge(T.sem.gi, 5)
     part = T.PK[:, 0:1]
-    v(ve.tensor_copy(T.IOH[:], T.IOF[:]))
-    v(ve.tensor_scalar(T.SEG[:], T.SEGF[:], 0.0, None, Op.is_gt))
-    v(ve.tensor_scalar(T.TM[:], T.IOF[:], part, -1.0, Op.is_le, Op.mult))
+    if head:
+        v(ve.tensor_copy(T.IOH[:], T.IOF[:]))
+        v(ve.tensor_scalar(T.TM[:], T.IOF[:], part, -1.0, Op.is_le, Op.mult))
+    else:
+        v(ve.tensor_scalar(T.IOH[:], T.IOF[:], -1.0, 128.0, Op.mult, Op.add))
+        v(ve.tensor_scalar(T.TM[:], T.IOF[:], part, -1.0, Op.is_lt, Op.mult))
+    edge = 128.0 if head else 129.0
+    v(ve.tensor_scalar(T.SEG[:, 0:4 * CC], T.SEGF[:, 0:4 * CC], 0.0, None, Op.is_gt))
     v(ve.tensor_scalar(T.ONEH[:], T.IOF[:], 0.0, None, Op.is_ge))
     v(ve.tensor_scalar(T.ID[:], T.IOF[:], part, None, Op.is_equal))
-    for k in range(8):
-        v(ve.tensor_scalar(T.WK[:, 128 * k:128 * k + 128], T.MODF[:], T.PK[:, k:k + 1], None, Op.is_equal))
+    if head:
+        for k in range(8):
+            v(ve.tensor_scalar(T.WK[:, 128 * k:128 * k + 128], T.MODF[:], T.PK[:, k:k + 1], None, Op.is_equal))
     if kind == "X":
         v(ve.memset(T.ONE32[:], 1.0))
         v(ve.memset(T.WIN[:, N * S:N * S + 8], 0.0))
-    else:
+    if kind in ("P", "W"):
+        v(ve.tensor_scalar(T.NID[:], T.IOF[:], part, 1.0 if head else -1.0, Op.is_equal, Op.mult))
         for x in range(N):
-            v(ve.tensor_scalar(T.IDX[:, 128 * x:128 * x + 128], T.IOF[:], part, float(S * x - S * N), Op.is_equal, Op.mult))
+            base = S * x if head else S * (x + 1)
+            v(ve.tensor_scalar(T.IDX[:, 128 * x:128 * x + 128], T.IOF[:], part, float(base - S * N), Op.is_equal, Op.mult))
 
-    this, other = (0, 16) if kind == "X" else (16, 0)
-    ve.wait_ge(T.sem.ld, 16 * BLK)
-    v(ve.tensor_scalar(T.HG[:], T.L[:], 12, None, Op.arith_shift_right))
-    v(ve.tensor_scalar(T.UV[:], T.L[:], 4095, None, Op.bitwise_and))
+    this, other = (0, 16) if kind in ("X", "Z") else (16, 0)
+    W2, W4 = 2 * CC, 4 * CC
+    ve.wait_ge(T.sem.ld, 16 * len(mine))
+    v(ve.tensor_scalar(T.HG[:, 0:W2], T.L[:, 0:W2], 12, None, Op.arith_shift_right))
+    v(ve.tensor_scalar(T.UV[:, 0:W2], T.L[:, 0:W2], 4095, None, Op.bitwise_and))
     ve.wait_ge(T.sem.v, n["v"] - 1)
-    v(ve.tensor_scalar(T.NOT[:], T.HG[:], float(r), 16.0, Op.not_equal, Op.mult))
+    v(ve.tensor_scalar(T.NOT[:, 0:W2], T.HG[:, 0:W2], float(r), 16.0, Op.not_equal, Op.mult))
     vw()
-    for k in range(6):
+    for k in range(CC // 16):
         v(ve.tensor_tensor(T.KEY[:, 16 * k:16 * k + 16], T.HG[:, 32 * k + other:32 * k + other + 16],
                            T.NOT[:, 32 * k + this:32 * k + this + 16], Op.add))
     vw()
-    W3 = 4 * C
     masked, scanned, placed, chosen = [], [], [], []
 
     def masks(i):
         for x in range(4 * i, 4 * i + 4):
-            v(ve.tensor_scalar(T.MR[:, C * x:C * x + C], T.KEY[:], float(x), None, Op.is_equal))
+            v(ve.tensor_scalar(T.MR[:, CC * x:CC * x + CC], T.KEY[:, 0:CC], float(x), None, Op.is_equal))
         masked.append(n["v"])
 
     def scan(i):
         ve.wait_ge(T.sem.v, masked[i])
-        scanned.append(v(ve.tensor_tensor_scan(T.SC[:, W3 * i:W3 * i + W3], T.SEG[:], T.MR[:, W3 * i:W3 * i + W3], 0.0, Op.mult, Op.add)))
+        scanned.append(v(ve.tensor_tensor_scan(T.SC[:, W4 * i:W4 * i + W4], T.SEG[:, 0:W4], T.MR[:, W4 * i:W4 * i + W4], 0.0, Op.mult, Op.add)))
 
     masks(0), masks(1), scan(0), masks(2), scan(1), scan(2)
-    v(ve.tensor_scalar(T.VAL[:], T.UV[:], -2048.0, None, Op.add))
+    v(ve.tensor_scalar(T.VAL[:, 0:W2], T.UV[:, 0:W2], -2048.0, None, Op.add))
     pos = [T.ps0, T.ps1, T.ps2]
     for i in range(3):
         pe.wait_ge(T.sem.v, masked[i])
-        t(pe.matmul(pos[i][:, 0:W3], T.TM[:], T.MR[:, W3 * i:W3 * i + W3], True, False))
+        t(pe.matmul(pos[i][:, 0:W4], T.TM[:], T.MR[:, W4 * i:W4 * i + W4], True, False))
         pe.wait_ge(T.sem.v, scanned[i])
-        placed.append(t(pe.matmul(pos[i][:, 0:W3], T.ONEH[:], T.SC[:, W3 * i:W3 * i + W3], False, True)))
+        placed.append(t(pe.matmul(pos[i][:, 0:W4], T.ONEH[:], T.SC[:, W4 * i:W4 * i + W4], False, True)))
     for i in range(3):
         ve.wait_ge(T.sem.t, placed[i])
-        chosen.append(v(ve.tensor_tensor(T.PROD[:, W3 * i:W3 * i + W3], T.MR[:, W3 * i:W3 * i + W3], pos[i][:, 0:W3], Op.mult)))
-    if kind == "P":
+        chosen.append(v(ve.tensor_tensor(T.PROD[:, W4 * i:W4 * i + W4], T.MR[:, W4 * i:W4 * i + W4], pos[i][:, 0:W4], Op.mult)))
+    if kind in ("P", "W"):
         for x in range(N):
-            t(pe.matmul(T.ps6[:, 0:C], T.IDX[:, 128 * x:128 * x + 128], T.MR[:, C * x:C * x + C], x == 0, False))
+            t(pe.matmul(T.ps6[:, 0:CC], T.IDX[:, 128 * x:128 * x + 128], T.MR[:, CC * x:CC * x + CC], x == 0, False))
     for x in range(N):
         if x % 4 == 0:
             pe.wait_ge(T.sem.v, chosen[x // 4])
-        t(pe.matmul(T.ps3[:, 0:C], T.ID[:], T.PROD[:, C * x:C * x + C], x == 0, x == N - 1))
+        t(pe.matmul(T.ps3[:, 0:CC], T.ID[:], T.PROD[:, CC * x:CC * x + CC], x == 0, x == N - 1))
     summed = n["t"]
-    if kind == "P":
+    if kind in ("P", "W"):
         for x in range(N):
-            t(pe.matmul(T.ps6[:, 0:C], T.ID[:], T.PROD[:, C * x:C * x + C], False, x == N - 1))
+            t(pe.matmul(T.ps6[:, 0:CC], T.NID[:], T.PROD[:, CC * x:CC * x + CC], False, x == N - 1))
     windowed = n["t"]
     vw()
     for i in range(3):
-        v(ve.tensor_scalar(T.MR[:, N * C + W3 * i:N * C + W3 * i + W3], T.PROD[:, W3 * i:W3 * i + W3], 128.0, None, Op.is_ge))
+        v(ve.tensor_scalar(T.MR[:, N * CC + W4 * i:N * CC + W4 * i + W4], T.PROD[:, W4 * i:W4 * i + W4], edge, None, Op.is_ge))
     ve.wait_ge(T.sem.t, summed)
-    v(ve.tensor_scalar(T.T1[:], T.ps3[:, 0:C], 128.0, -128.0, Op.is_ge, Op.mult))
+    v(ve.tensor_scalar(T.T1[:, 0:CC], T.ps3[:, 0:CC], edge, -128.0, Op.is_ge, Op.mult))
     vw()
-    v(ve.tensor_tensor(T.ROW[:], T.T1[:], T.ps3[:, 0:C], Op.add))
+    v(ve.tensor_tensor(T.ROW[:, 0:CC], T.T1[:, 0:CC], T.ps3[:, 0:CC], Op.add))
     vw()
-    for c in range(C):
-        if kind == "P" and c == 24:
-            ve.wait_ge(T.sem.t, windowed)
-            g.wait_ge(T.sem.v, v(ve.tensor_scalar(T.OD[:], T.ps6[:, 0:C], float(S * N), None, Op.add)))
-            write(T.OD[:], T.OD[:], X[r], "od", off_chip)
-        w = 32 * (c // 16) + this + c % 16
-        hot = T.HOT[:, 128 * c:128 * c + 128]
-        v(ve.tensor_scalar(hot, T.IOH[:], T.ROW[:, c:c + 1], T.VAL[:, w:w + 1], Op.is_equal, Op.mult))
-        pe.wait_ge(T.sem.v, n["v"])
-        t(pe.matmul(T.ps4[:, 0:24], hot, T.MR[:, c:2 * N * C:C], c == 0, c == C - 1))
+
+    def table(bank, out):
+        ve.wait_ge(T.sem.t, n["t"])
+        lo, hi = (0, 1) if head else (1, 0)
+        v(ve.tensor_copy(out[:, hi:24:2], bank[:, 12:24]))
+        vw()
+        return v(ve.tensor_tensor(out[:, lo:24:2], bank[:, 0:12], out[:, hi:24:2], Op.subtract))
+
+    stops = [CC // 2, CC] if kind == "Z" else [CC]
+    begin = 0
+    for k, stop in enumerate(stops):
+        bank = (T.ps4, T.ps7)[k]
+        for c in range(begin, stop):
+            if kind in ("P", "W") and c == CC // 4:
+                ve.wait_ge(T.sem.t, windowed)
+                g.wait_ge(T.sem.v, v(ve.tensor_scalar(T.OD[:, 0:CC], T.ps6[:, 0:CC], float(S * N), None, Op.add)))
+                c0 = 32 * mine[0]
+                write(T.OD[:, c0:c0 + CC], T.OD[:, 0:CC], X[r], "od", off_chip)
+            w = 32 * (c // 16) + this + c % 16
+            hot = T.HOT[:, 128 * c:128 * c + 128]
+            v(ve.tensor_scalar(hot, T.IOH[:], T.ROW[:, c:c + 1], T.VAL[:, w:w + 1], Op.is_equal, Op.mult))
+            pe.wait_ge(T.sem.v, n["v"])
+            t(pe.matmul(bank[:, 0:24], hot, T.MR[:, c:2 * N * CC:CC], c == begin, c == stop - 1))
+        begin = stop
+        filled = table(bank, (T.PF, T.PG)[k])
+        if not head:
+            g.wait_ge(T.sem.v, filled)
+            write((T.PT0, T.PT1)[k][:], (T.PF, T.PG)[k][:], near, "pt%d" % k, off_chip)
+    if not head:
+        g.wait_ge(T.sem.ls, n["ls"])
+        return
     out = T.OA if kind == "X" else T.OB
-    ve.wait_ge(T.sem.t, n["t"])
-    v(ve.tensor_copy(T.PF[:, 1:24:2], T.ps4[:, 12:24]))
-    vw()
-    v(ve.tensor_tensor(T.PF[:, 0:24:2], T.ps4[:, 0:12], T.PF[:, 1:24:2], Op.subtract))
+    whole = T.PF
+    for k, more in enumerate((T.PT0, T.PT1) if kind == "X" else (T.PT0,)):
+        vw()
+        ve.wait_ge(T.sem["pt%d" % k], len(off_chip))
+        v(ve.tensor_tensor((T.PS, T.PG)[k][:], whole[:], more[:], Op.add))
+        whole = (T.PS, T.PG)[k]
     pe.wait_ge(T.sem.v, n["v"])
     for k in range(8):
-        t(pe.matmul(T.ps5[:, k:192:8], T.WK[:, 128 * k:128 * k + 128], T.PF[:], True, True))
+        t(pe.matmul(T.ps5[:, k:192:8], T.WK[:, 128 * k:128 * k + 128], whole[:], True, True))
     ve.wait_ge(T.sem.t, n["t"])
     listed = v(ve.tensor_scalar(out[:], T.ps5[:, 0:192], 2048.0, None, Op.add))
 
@@ -273,10 +329,9 @@ def rank_program(g, core, T, topo):
         g.wait_ge(T.sem.ls, n["ls"])
         return
 
-    ve.wait_ge(T.sem.lta, 16)
-    ve.wait_ge(T.sem.v, listed)
-    sc.wait_ge(T.sem.lta, 16)
-    sc.wait_ge(T.sem.v, listed)
+    for q in (ve, sc):
+        q.wait_ge(T.sem.lta, 32)
+        q.wait_ge(T.sem.v, listed)
     helped = [d for ds in HELPED for d in ds]
     straight = [d for ds in STRAIGHT for d in ds]
     got = {}
@@ -331,7 +386,7 @@ def rank_program(g, core, T, topo):
         copied.append(a(sc.activation(T.WIN[:, S * s:S * s + S], banks[k % 8][:, 0:S], Fn.Copy)))
     for q in (ve, sc):
         q.wait_ge(T.sem.a, n["a"])
-        q.wait_ge(T.sem.od, len(off_chip))
+        q.wait_ge(T.sem.od, 2 * len(off_chip))
 
     def spread(engine, c0, c1):
         o, w = T.D[:, 16 * c0:16 * c1], T.WIN[:, 0:N * S + 8].indirect(T.OD[:, c0:c1])

from concourse.bass import DstId, RemoteDMATransfer
from concourse.mybir import AxisListType
from concourse.mybir import AluOpType as Op
from concourse.mybir import ActivationFunctionType as Fn

N = 12
C = 96
S = 256
BLK = 3
HEAD = 2
WORLD = 256
STRAIGHT = ((2, 10), (4, 8), (1, 11))
HELPED = ((3,), (9, 5), (7, 6))
CALLS = ((0, 1, 2, 3, 4, 5, 6, 7), (8, 9, 10, 11))
EARLY = 1280

SCRATCH = {
    "LAND": ("dram", [N, 128, 16], "int32"),
    "RET": ("dram", [N, 128, 8], "float32"),
    "BACK": ("dram", [N, 128, 8], "float32"),
    "TAS": ("sbuf", [128, 4096], "float32"),
    "TBS": ("sbuf", [128, 4096], "float32"),
    "L": ("sbuf", [128, 128], "int32"),
    "HG": ("sbuf", [128, 128], "int32"),
    "UV": ("sbuf", [128, 128], "int32"),
    "VAL": ("sbuf", [128, 128], "float32"),
    "NOT": ("sbuf", [128, 128], "float16"),
    "KEY": ("sbuf", [128, C], "float16"),
    "MR": ("sbuf", [128, 2 * N * C], "float16"),
    "SC": ("sbuf", [128, N * C], "float16"),
    "PROD": ("sbuf", [128, N * C], "float16"),
    "T1": ("sbuf", [128, C], "float32"),
    "ROW": ("sbuf", [128, C], "float32"),
    "HOT": ("sbuf", [128, 64 * 128], "float16"),
    "PF": ("sbuf", [128, 24], "float16"),
    "PG": ("sbuf", [128, 24], "float16"),
    "PT0": ("sbuf", [128, 24], "float16"),
    "PT1": ("sbuf", [128, 24], "float16"),
    "PS": ("sbuf", [128, 24], "float16"),
    "OA": ("sbuf", [128, 192], "uint16"),
    "OB": ("sbuf", [128, 192], "uint16"),
    "OD": ("sbuf", [128, C], "uint16"),
    "COL": ("sbuf", [128, 11 * S], "float32"),
    "FWD": ("sbuf", [128, 5 * S], "float32"),
    "RECV": ("sbuf", [128, N * S], "float32"),
    "PR": ("sbuf", [128, N * S], "float32"),
    "WIN": ("sbuf", [128, N * S + 8], "float32"),
    "D": ("sbuf", [128, 16 * C], "float32"),
    "FIN": ("sbuf", [96, 516], "float32"),
    "Y": ("sbuf", [32, 32], "float32"),
    "IOF": ("sbuf", [128, 128], "float32"),
    "IOH": ("sbuf", [128, 128], "float16"),
    "PK": ("sbuf", [128, 8], "float32"),
    "MODF": ("sbuf", [128, 128], "float32"),
    "SEGF": ("sbuf", [128, 256], "float32"),
    "SEG": ("sbuf", [128, 256], "float16"),
    "PI1": ("sbuf", [128, 1], "int32"),
    "PI2": ("sbuf", [128, 1], "int32"),
    "PF2": ("sbuf", [128, 1], "float32"),
    "GE": ("sbuf", [128, 4], "float32"),
    "TM": ("sbuf", [128, 128], "float16"),
    "ONEH": ("sbuf", [128, 128], "float16"),
    "ID": ("sbuf", [128, 128], "float16"),
    "NID": ("sbuf", [128, 128], "float16"),
    "WK": ("sbuf", [128, 8 * 128], "float16"),
    "IDX": ("sbuf", [128, N * 128], "float16"),
    "ONE32": ("sbuf", [128, 128], "float32"),
    "Z": ("sbuf", [128, 48], "float32"),
}
for _i in range(8):
    SCRATCH["ps%d" % _i] = ("psum", [128, 512], "float32")

SEMAPHORES = (["v", "t", "a", "gi", "own", "lst", "ld", "lta", "ltb", "ob", "od", "pt0", "pt1", "ls", "bk", "back", "fin", "st"]
              + ["rd%d" % j for j in range(BLK)] + ["fw%d" % k for k in range(len(HELPED))] + ["col%d" % a for a in range(N)])


def bits(mask):
    return [e for e in range(16) if mask >> e & 1]


def mask_of(engines):
    m = 0
    for e in engines:
        m |= 1 << e
    return m


def same_chip(a, b, topo):
    return topo.host(a) == topo.host(b) and topo.chip(a) == topo.chip(b)


def helper(x, cores, topo):
    for c in range(WORLD):
        if same_chip(c, x, topo) and topo.die(c) != topo.die(x) and all(topo.may_write(c, d) for d in cores if d != c):
            return c


def beside(x, topo):
    for c in range(WORLD):
        if c != x and same_chip(c, x, topo) and topo.die(c) == topo.die(x):
            return c


def split(engines, n):
    w = len(engines) // n
    return [engines[w * k:w * k + w] for k in range(n)]


def rank_program(g, core, T, topo):
    X = list(T.cores)
    r = None
    for q, x in enumerate(X):
        if same_chip(core, x, topo):
            r = q
    if r is None:
        return
    P = [helper(x, X, topo) for x in X]
    Z = [beside(x, topo) for x in X]
    W = [beside(p, topo) for p in P]
    kind = None
    for name, group in (("X", X), ("P", P), ("Z", Z), ("W", W)):
        if core == group[r]:
            kind = name
    if kind is None:
        return
    head = kind in ("X", "P")
    far = next(x for x in X if topo.may_write(core, x) and not same_chip(x, core, topo))
    off_chip = bits(topo.mask(core, far))
    near = {"X": P, "P": X, "Z": X, "W": P}[kind][r]
    inner = [e for e in bits(topo.mask(core, near)) if e not in off_chip]
    ve, pe, sc, sy = g.vector, g.tensor, g.scalar, g.sync
    n = {"v": 0, "t": 0, "a": 0, "ls": 0}

    def v(ins):
        n["v"] += 1
        ins.then_inc(T.sem.v, 1)
        return n["v"]

    def t(ins):
        n["t"] += 1
        ins.then_inc(T.sem.t, 1)
        return n["t"]

    def a(ins):
        n["a"] += 1
        ins.then_inc(T.sem.a, 1)
        return n["a"]

    def vw():
        ve.wait_ge(T.sem.v, n["v"])

    def dst(d):
        rid, pid = topo.addr(d, core)
        return DstId(rid=rid, pnc=pid)

    def write(out, src, d, sem, engines):
        rid, pid = topo.addr(d, core)
        g.remote_dma(out, src, T.sem[sem], T.sem.ls, pid, rid, mask_of(engines))
        n["ls"] += len(engines)

    def cast(group):
        tr = []
        for ds, es in (([d for d in group if not same_chip(d, core, topo)], off_chip),
                       ([d for d in group if same_chip(d, core, topo) and d != core], inner)):
            if ds:
                tr.append(RemoteDMATransfer(src=T.LAND[r], dsts=[T.LAND[r] for d in ds], dst_ids=[dst(d) for d in ds],
                                            dma_engine_mask=mask_of(es), remote_sem=T.sem.lst))
                n["ls"] += len(es)
        g.remote_dma_fused(tr, local_sem=T.sem.ls)

    mine = list(range(HEAD)) if head else list(range(HEAD, BLK))
    CC = 32 * len(mine)
    lists = [4 * j + k for j in mine for k in range(4)]
    ours = kind == "X" and r in lists
    if kind == "X":
        sy.dma_start(T.LAND[r, 0:128:2, :], T.pi[:]).then_inc(T.sem.own, 16)
        sc.dma_start(T.LAND[r, 1:128:2, :], T.pj[:]).then_inc(T.sem.own, 16)
        sy.dma_start(T.TAS[:, 0:EARLY], T.ta[:, 0:EARLY]).then_inc(T.sem.lta, 16)
    F = {"allow_small_or_imprecise_dtypes": True}
    g.iota(T.IOF[:], [[1, 128]], 0, 0, **F).then_inc(T.sem.gi, 1)
    g.iota(T.PK[:], [[-16, 8]], 0, 1, **F).then_inc(T.sem.gi, 1)
    g.iota(T.MODF[:], [[0, 8], [1, 16]], 0, 0, **F).then_inc(T.sem.gi, 1)
    g.iota(T.PI1[:], [[0, 1]], 0, 1).then_inc(T.sem.gi, 1)
    if kind == "X":
        g.wait_ge(T.sem.own, 32)
        for group in ((X, P) if r < 4 * HEAD else (Z, W)):
            cast(group)
    g.iota(T.SEGF[:, 0:4 * CC], [[0, 4], [1, CC]], 0, 0, **F).then_inc(T.sem.gi, 1)
    if ours:
        sy.wait_ge(T.sem.own, 32)
    sy.wait_ge(T.sem.lst, sum(len(inner) if same_chip(X[q], core, topo) else len(off_chip) for q in lists if not (ours and q == r)))
    for k, j in enumerate(mine):
        sy.dma_start(T.L[:, 64 * k:64 * k + 64], T.LAND[4 * j:4 * j + 4]).then_inc(T.sem.ld, 16)
    if kind == "X":
        sy.dma_start(T.TAS[:, EARLY:4096], T.ta[:, EARLY:4096]).then_inc(T.sem.lta, 16)
        sy.dma_start(T.TBS[:], T.tb[:]).then_inc(T.sem.ltb, 16)

    ve.wait_ge(T.sem.gi, 5)
    part = T.PK[:, 0:1]
    if head:
        v(ve.tensor_copy(T.IOH[:], T.IOF[:]))
        v(ve.tensor_scalar(T.TM[:], T.IOF[:], part, -1.0, Op.is_le, Op.mult))
    else:
        v(ve.tensor_scalar(T.IOH[:], T.IOF[:], -1.0, 128.0, Op.mult, Op.add))
        v(ve.tensor_scalar(T.TM[:], T.IOF[:], part, -1.0, Op.is_lt, Op.mult))
    edge = 128.0 if head else 129.0
    v(ve.tensor_scalar(T.SEG[:, 0:4 * CC], T.SEGF[:, 0:4 * CC], 0.0, None, Op.is_gt))
    v(ve.tensor_scalar(T.ONEH[:], T.IOF[:], 0.0, None, Op.is_ge))
    v(ve.tensor_scalar(T.ID[:], T.IOF[:], part, None, Op.is_equal))
    if head:
        for k in range(8):
            v(ve.tensor_scalar(T.WK[:, 128 * k:128 * k + 128], T.MODF[:], T.PK[:, k:k + 1], None, Op.is_equal))
    if kind == "X":
        v(ve.memset(T.ONE32[:], 1.0))
        v(ve.memset(T.WIN[:, N * S:N * S + 8], 0.0))
    if kind in ("P", "W"):
        v(ve.tensor_scalar(T.NID[:], T.IOF[:], part, 1.0 if head else -1.0, Op.is_equal, Op.mult))
        for x in range(N):
            base = S * x if head else S * (x + 1)
            v(ve.tensor_scalar(T.IDX[:, 128 * x:128 * x + 128], T.IOF[:], part, float(base - S * N), Op.is_equal, Op.mult))

    this, other = (0, 16) if kind in ("X", "Z") else (16, 0)
    W2, W4 = 2 * CC, 4 * CC
    ve.wait_ge(T.sem.ld, 16 * len(mine))
    v(ve.tensor_scalar(T.HG[:, 0:W2], T.L[:, 0:W2], 12, None, Op.arith_shift_right))
    v(ve.tensor_scalar(T.UV[:, 0:W2], T.L[:, 0:W2], 4095, None, Op.bitwise_and))
    ve.wait_ge(T.sem.v, n["v"] - 1)
    v(ve.tensor_scalar(T.NOT[:, 0:W2], T.HG[:, 0:W2], float(r), 16.0, Op.not_equal, Op.mult))
    vw()
    for k in range(CC // 16):
        v(ve.tensor_tensor(T.KEY[:, 16 * k:16 * k + 16], T.HG[:, 32 * k + other:32 * k + other + 16],
                           T.NOT[:, 32 * k + this:32 * k + this + 16], Op.add))
    vw()
    masked, scanned, placed, chosen = [], [], [], []

    def masks(i):
        for x in range(4 * i, 4 * i + 4):
            v(ve.tensor_scalar(T.MR[:, CC * x:CC * x + CC], T.KEY[:, 0:CC], float(x), None, Op.is_equal))
        masked.append(n["v"])

    def scan(i):
        ve.wait_ge(T.sem.v, masked[i])
        scanned.append(v(ve.tensor_tensor_scan(T.SC[:, W4 * i:W4 * i + W4], T.SEG[:, 0:W4], T.MR[:, W4 * i:W4 * i + W4], 0.0, Op.mult, Op.add)))

    masks(0), masks(1), scan(0), masks(2), scan(1), scan(2)
    v(ve.tensor_scalar(T.VAL[:, 0:W2], T.UV[:, 0:W2], -2048.0, None, Op.add))
    pos = [T.ps0, T.ps1, T.ps2]
    for i in range(3):
        pe.wait_ge(T.sem.v, masked[i])
        t(pe.matmul(pos[i][:, 0:W4], T.TM[:], T.MR[:, W4 * i:W4 * i + W4], True, False))
        pe.wait_ge(T.sem.v, scanned[i])
        placed.append(t(pe.matmul(pos[i][:, 0:W4], T.ONEH[:], T.SC[:, W4 * i:W4 * i + W4], False, True)))
    for i in range(3):
        ve.wait_ge(T.sem.t, placed[i])
        chosen.append(v(ve.tensor_tensor(T.PROD[:, W4 * i:W4 * i + W4], T.MR[:, W4 * i:W4 * i + W4], pos[i][:, 0:W4], Op.mult)))
    if kind in ("P", "W"):
        for x in range(N):
            t(pe.matmul(T.ps6[:, 0:CC], T.IDX[:, 128 * x:128 * x + 128], T.MR[:, CC * x:CC * x + CC], x == 0, False))
    for x in range(N):
        if x % 4 == 0:
            pe.wait_ge(T.sem.v, chosen[x // 4])
        t(pe.matmul(T.ps3[:, 0:CC], T.ID[:], T.PROD[:, CC * x:CC * x + CC], x == 0, x == N - 1))
    summed = n["t"]
    if kind in ("P", "W"):
        for x in range(N):
            t(pe.matmul(T.ps6[:, 0:CC], T.NID[:], T.PROD[:, CC * x:CC * x + CC], False, x == N - 1))
    windowed = n["t"]
    vw()
    for i in range(3):
        v(ve.tensor_scalar(T.MR[:, N * CC + W4 * i:N * CC + W4 * i + W4], T.PROD[:, W4 * i:W4 * i + W4], edge, None, Op.is_ge))
    ve.wait_ge(T.sem.t, summed)
    v(ve.tensor_scalar(T.T1[:, 0:CC], T.ps3[:, 0:CC], edge, -128.0, Op.is_ge, Op.mult))
    vw()
    v(ve.tensor_tensor(T.ROW[:, 0:CC], T.T1[:, 0:CC], T.ps3[:, 0:CC], Op.add))
    vw()

    def table(bank, out):
        ve.wait_ge(T.sem.t, n["t"])
        lo, hi = (0, 1) if head else (1, 0)
        v(ve.tensor_copy(out[:, hi:24:2], bank[:, 12:24]))
        vw()
        return v(ve.tensor_tensor(out[:, lo:24:2], bank[:, 0:12], out[:, hi:24:2], Op.subtract))

    stops = [CC // 2, CC] if kind == "Z" else [CC]
    begin = 0
    for k, stop in enumerate(stops):
        bank = (T.ps4, T.ps7)[k]
        for c in range(begin, stop):
            if kind in ("P", "W") and c == CC // 4:
                ve.wait_ge(T.sem.t, windowed)
                g.wait_ge(T.sem.v, v(ve.tensor_scalar(T.OD[:, 0:CC], T.ps6[:, 0:CC], float(S * N), None, Op.add)))
                c0 = 32 * mine[0]
                write(T.OD[:, c0:c0 + CC], T.OD[:, 0:CC], X[r], "od", off_chip)
            w = 32 * (c // 16) + this + c % 16
            hot = T.HOT[:, 128 * c:128 * c + 128]
            v(ve.tensor_scalar(hot, T.IOH[:], T.ROW[:, c:c + 1], T.VAL[:, w:w + 1], Op.is_equal, Op.mult))
            pe.wait_ge(T.sem.v, n["v"])
            t(pe.matmul(bank[:, 0:24], hot, T.MR[:, c:2 * N * CC:CC], c == begin, c == stop - 1))
        begin = stop
        filled = table(bank, (T.PF, T.PG)[k])
        if not head:
            g.wait_ge(T.sem.v, filled)
            write((T.PT0, T.PT1)[k][:], (T.PF, T.PG)[k][:], near, "pt%d" % k, off_chip)
    if not head:
        g.wait_ge(T.sem.ls, n["ls"])
        return
    out = T.OA if kind == "X" else T.OB
    whole = T.PF
    for k, more in enumerate((T.PT0, T.PT1) if kind == "X" else (T.PT0,)):
        vw()
        ve.wait_ge(T.sem["pt%d" % k], len(off_chip))
        v(ve.tensor_tensor((T.PS, T.PG)[k][:], whole[:], more[:], Op.add))
        whole = (T.PS, T.PG)[k]
    pe.wait_ge(T.sem.v, n["v"])
    for k in range(8):
        t(pe.matmul(T.ps5[:, k:192:8], T.WK[:, 128 * k:128 * k + 128], whole[:], True, True))
    ve.wait_ge(T.sem.t, n["t"])
    listed = v(ve.tensor_scalar(out[:], T.ps5[:, 0:192], 2048.0, None, Op.add))

    if kind == "P":
        g.wait_ge(T.sem.v, listed)
        write(T.OB[:], T.OB[:], X[r], "ob", off_chip)
        at = 0
        for k, ds in enumerate(HELPED):
            g.wait_ge(T.sem["fw%d" % k], len(inner))
            for d in ds:
                write(T.RECV[:, S * r:S * r + S], T.FWD[:, S * at:S * at + S], X[(r + d) % N], "col%d" % r, off_chip)
                at += 1
        g.wait_ge(T.sem.ls, n["ls"])
        return

    for q in (ve, sc):
        q.wait_ge(T.sem.lta, 32)
        q.wait_ge(T.sem.v, listed)
    helped = [d for ds in HELPED for d in ds]
    straight = [d for ds in STRAIGHT for d in ds]
    got = {}
    for k, d in enumerate(helped):
        b = (r + d) % N
        got[d] = v(ve.tensor_copy(T.COL[:, S * k:S * k + S], T.TAS[:, 0:4096].indirect(T.OA[:, 16 * b:16 * b + 16])))
    for k, d in enumerate(straight):
        b, at = (r + d) % N, len(helped) + k
        got[d] = a(sc.activation(T.COL[:, S * at:S * at + S], T.TAS[:, 0:4096].indirect(T.OA[:, 16 * b:16 * b + 16]), Fn.Copy))
    own = a(sc.activation(T.RECV[:, S * r:S * r + S], T.TAS[:, 0:4096].indirect(T.OA[:, 16 * r:16 * r + 16]), Fn.Copy))
    at, to = 0, len(helped)
    for k in range(len(HELPED)):
        g.wait_ge(T.sem.v, got[HELPED[k][-1]])
        w = len(HELPED[k])
        write(T.FWD[:, S * at:S * (at + w)], T.COL[:, S * at:S * (at + w)], P[r], "fw%d" % k, inner)
        at += w
        g.wait_ge(T.sem.a, got[STRAIGHT[k][-1]])
        parts = split(off_chip, len(STRAIGHT[k]))
        g.remote_dma_fused([RemoteDMATransfer(src=T.COL[:, S * (to + m):S * (to + m + 1)], dst=T.RECV[:, S * r:S * r + S],
                                              dst_ids=[dst(X[(r + d) % N])], dma_engine_mask=mask_of(parts[m]),
                                              remote_sem=T.sem["col%d" % r]) for m, d in enumerate(STRAIGHT[k])], local_sem=T.sem.ls)
        n["ls"] += sum(len(p) for p in parts)
        to += len(STRAIGHT[k])

    v(ve.tensor_scalar(T.PI2[:], T.PI1[:], 1, None, Op.bitwise_and))
    for f in range(1, 4):
        v(ve.tensor_scalar(T.GE[:, f:f + 1], part, 24.0 * f, None, Op.is_ge))
    vw()
    v(ve.tensor_scalar(T.PF2[:], T.PI2[:], 16.0, 12.0, Op.mult, Op.add))
    v(ve.tensor_reduce(T.GE[:, 0:1], T.GE[:, 1:4], AxisListType.X, Op.add))
    vw()
    v(ve.tensor_scalar(T.Z[:], T.IOF[:, 0:48], T.PF2[:, 0:1], T.GE[:, 0:1], Op.subtract, Op.is_equal))

    ve.wait_ge(T.sem.ltb, 16)
    ve.wait_ge(T.sem.ob, len(off_chip))
    banks = [T.ps0, T.ps1, T.ps2, T.ps3, T.ps4, T.ps5, T.ps6, T.ps7]
    turn = [(0, 0)]
    for k in range(len(HELPED)):
        turn += [(d, len(off_chip) // len(STRAIGHT[k])) for d in STRAIGHT[k]] + [(d, len(off_chip)) for d in HELPED[k]]
    copied = []
    for k, (d, e) in enumerate(turn):
        s = (r - d) % N
        if d == 0:
            ve.wait_ge(T.sem.a, own)
        else:
            ve.wait_ge(T.sem["col%d" % s], e)
        blk = T.PR[:, S * s:S * s + S]
        pe.wait_ge(T.sem.v, v(ve.tensor_tensor(blk, T.TBS[:, 0:4096].indirect(T.OB[:, 16 * s:16 * s + 16]), T.RECV[:, S * s:S * s + S], Op.mult)))
        if k >= 8:
            pe.wait_ge(T.sem.a, copied[k - 8])
        sc.wait_ge(T.sem.t, t(pe.matmul(banks[k % 8][:, 0:S], T.ONE32[:], blk, True, True)))
        copied.append(a(sc.activation(T.WIN[:, S * s:S * s + S], banks[k % 8][:, 0:S], Fn.Copy)))
    for q in (ve, sc):
        q.wait_ge(T.sem.a, n["a"])
        q.wait_ge(T.sem.od, 2 * len(off_chip))

    def spread(engine, c0, c1):
        o, w = T.D[:, 16 * c0:16 * c1], T.WIN[:, 0:N * S + 8].indirect(T.OD[:, c0:c1])
        return v(ve.tensor_copy(o, w)) if engine == "v" else a(sc.activation(o, w, Fn.Copy))

    done = [{"v": spread("v", 0, 32)}, {"a": spread("a", 32, 64)}, {"v": spread("v", 64, 80), "a": spread("a", 80, 96)}]

    def after(queue, j):
        for name in done[j]:
            queue.wait_ge(T.sem[name], done[j][name])

    for j in range(BLK):
        after(sy, j)
        sy.dma_start(T.RET[4 * j:4 * j + 4], T.D[0:128:16, 512 * j:512 * j + 512]).then_inc(T.sem["rd%d" % j], 16)
    for qs in CALLS:
        for j in sorted({q // 4 for q in qs}):
            g.wait_ge(T.sem["rd%d" % j], 16)
        w = len(off_chip) // len(qs)
        tr = [RemoteDMATransfer(src=T.RET[q], dst=T.BACK[r], dst_ids=[dst(X[q])], remote_sem=T.sem.back,
                                dma_engine_mask=mask_of(off_chip[w * k:w * k + w])) for k, q in enumerate(qs) if q != r]
        g.remote_dma_fused(tr, local_sem=T.sem.ls)
        n["ls"] += w * len(tr)
    j, p0 = r // 4, 32 * (r % 4)
    after(sc, j)
    sc.dma_start(T.BACK[r], T.D[p0:p0 + 32:16, 512 * j:512 * j + 512]).then_inc(T.sem.bk, 16)
    w = next(len(off_chip) // len(qs) for qs in CALLS if r in qs)
    for q in (sy, sc):
        q.wait_ge(T.sem.bk, 16)
        q.wait_ge(T.sem.back, (N - 1) * w)
    for f in range(4):
        (sy, sc)[f % 2].dma_start(T.FIN[24 * f:24 * f + 24, 3 - f:515 - f], T.BACK[:]).then_inc(T.sem.fin, 16)
    pe.wait_ge(T.sem.fin, 64)
    pe.wait_ge(T.sem.a, copied[8])
    for k in range(4):
        t(pe.matmul(T.ps0[0:32, 0:32], T.Z[0:96, 12 - 4 * k:44 - 4 * k], T.FIN[0:96, 3 + 4 * k:512:16], k == 0, k == 3))
    ve.wait_ge(T.sem.t, n["t"])
    v(ve.tensor_copy(T.Y[:], T.ps0[0:32, 0:32]))
    sy.wait_ge(T.sem.v, n["v"])
    sy.dma_start(T.y[:], T.Y[:]).then_inc(T.sem.st, 16)
    sy.wait_ge(T.sem.st, 16)
    g.wait_ge(T.sem.ls, n["ls"])
